import numpy as np
import ml_dtypes


def mxq(x, axis, fmt="e4m3"):
    dtype, down = {"e4m3": (ml_dtypes.float8_e4m3fn, 7), "e5m2": (ml_dtypes.float8_e5m2, 14)}[fmt]
    v = np.moveaxis(np.asarray(x, np.float32).astype(ml_dtypes.bfloat16).astype(np.float64), axis, -1)
    blocks = v.reshape(v.shape[:-1] + (-1, 32))
    amax = np.abs(blocks).max(-1, keepdims=True)
    byte = np.maximum(np.where(amax > 0, np.frexp(amax)[1] - 1 + 127, 0) - down, 1)
    scale = np.exp2(byte - 127.0)
    codes = (blocks / scale).astype(np.float32).astype(dtype).astype(np.float64)
    return np.moveaxis((codes * scale).reshape(v.shape), -1, axis)


WIDE = False


def mx_kscale(k):
    if not WIDE:
        return np.ones(k)
    levels = np.array([10, -10, 5, -5, 0])
    if k % 512:
        return np.exp2(np.random.permutation(np.resize(levels, k // 32))).repeat(32)
    a = np.empty((k // 512, 16))
    for p in range(k // 512):
        a[p, :8] = np.random.permutation(np.resize(levels, 8))
        for g in range(8):
            far = levels[np.abs(levels - a[p, g]) >= 10]
            a[p, g + 8] = far[np.random.randint(len(far))]
    return np.exp2(a.ravel()).repeat(32)


def f64(x):
    return np.asarray(x).astype(np.float64)


def striped(idx):
    return np.tile(idx.reshape(-1, 16).T, (8, 1)).astype(np.uint16)


def unstriped(offs):
    return offs[:16].T.reshape(-1).astype(np.int64)


def relu2(v):
    return np.maximum(v, 0.0) ** 2


K, T, D, S, V, N = 512, 1024, 2, 512, 256, 512


def setup_inputs():
    n = np.random.standard_normal
    s = mx_kscale(K)[:, None]
    return {
        "xT": (n((K, T)) * s).astype(np.float32),
        "w": (n((D, K, N)) / np.sqrt(D * K) / s[None]).astype(np.float32),
        "b": (0.3 * n((N, 1))).astype(np.float32),
        "gate": np.tile(np.random.uniform(0.2, 1.0, S), (N, 1)).astype(np.float32),
        "offs": striped(np.random.permutation(T)[:S]),
    }


def reference(xT, w, b, gate, offs):
    idx = unstriped(offs)
    xq = mxq(f64(xT)[:, idx], 0, "e4m3")
    wq = mxq(f64(w), 1, "e4m3")
    y = sum(wq[d].T @ xq[:, d * V:(d + 1) * V] for d in range(D))
    y = relu2(y + f64(b))
    out = np.zeros((N, T))
    out[:, idx] = f64(gate) * np.tile(y, (1, D))
    return out

@@ -1,0 +1,206 @@
+from contextlib import ExitStack
+
+import concourse.mybir as mybir
+
+K, T, D, S, V, N = 512, 1024, 2, 512, 256, 512
+FLOPS = 2 * D * K * N * V
+
+F32 = mybir.dt.float32
+BF16 = mybir.dt.bfloat16
+U32 = mybir.dt.uint32
+U16 = mybir.dt.uint16
+U8 = mybir.dt.uint8
+FP8X4 = mybir.dt.float8_e4m3fn_x4
+ACT = mybir.ActivationFunctionType
+MULT = mybir.AluOpType.mult
+
+P = 128
+PACK = 4
+BLOCKS = N // P
+HALF = V // 2
+PER_COL = 16
+
+
+def interleave_views(dst, src):
+    return (
+        dst.rearrange("p (c i) t -> p c t i", i=4),
+        src.rearrange("p t (c i) -> p c t i", i=4),
+    )
+
+
+def interleave_scalar(nc, dst, src):
+    o, i = interleave_views(dst, src)
+    nc.scalar.activation(out=o, in_=i, func=ACT.Copy)
+
+
+def interleave_vector(nc, dst, src):
+    o, i = interleave_views(dst, src)
+    nc.vector.tensor_copy(out=o, in_=i)
+
+
+def tile_picked_tome_lin_relu2_sub_e_kernel(tc, xT, w, b, gate, offs, out):
+    nc = tc.nc
+    with ExitStack() as ctx:
+        keep = ctx.enter_context(tc.tile_pool(name="keep", bufs=1))
+        work = ctx.enter_context(tc.tile_pool(name="work", bufs=1))
+        psum = ctx.enter_context(tc.psum_pool(name="psum", bufs=1))
+
+        offsets = keep.tile([P, S // PER_COL], U16, name="offsets")
+        nc.sync.dma_start(offsets[:], offs)
+
+        def entries(a, z):
+            return offsets[:, a // PER_COL : z // PER_COL]
+
+        x_rows = xT.rearrange("(p j) t -> p j t", j=PACK)
+        planes = [keep.tile([P, T], F32, name=f"plane{j}") for j in range(PACK)]
+        for j in range(PACK):
+            nc.sync.dma_start(out=planes[j][:], in_=x_rows[:, j, :])
+
+        w_rows = [w[d].rearrange("(p j) m -> p j m", j=PACK) for d in range(D)]
+        w_raw = [[keep.tile([P, PACK, P], F32, name=f"w_raw{c}_{d}") for d in range(D)] for c in range(2)]
+        w_late = [keep.tile([P, PACK, 2 * P], F32, name=f"w_late{d}") for d in range(D)]
+        gates = keep.tile([P, BLOCKS, S], F32, name="gates")
+        gate_rows = gate.rearrange("(c p) s -> p c s", p=P)
+        bias = keep.tile([P, BLOCKS], F32, name="bias")
+
+        for d in range(D):
+            nc.sync.dma_start(out=w_raw[0][d][:], in_=w_rows[d][:, :, 0:P])
+        with nc.allow_non_contiguous_dma(reason="one bias value a partition"):
+            nc.sync.dma_start(out=bias[:], in_=b.rearrange("(c p) o -> p (c o)", p=P))
+        for d in range(D):
+            nc.sync.dma_start(out=w_raw[1][d][:], in_=w_rows[d][:, :, P : 2 * P])
+            nc.sync.dma_start(out=gates[:, 0, d * V : (d + 1) * V], in_=gate_rows[:, 0, d * V : (d + 1) * V])
+        for d in range(D):
+            nc.sync.dma_start(out=w_late[d][:], in_=w_rows[d][:, :, 2 * P : 4 * P])
+        nc.sync.dma_start(out=gates[:, 1:4, :], in_=gate_rows[:, 1:4, :])
+
+        def w_source(c, d):
+            if c < 2:
+                return w_raw[c][d][:]
+            return w_late[d][:, :, (c - 2) * P : (c - 1) * P]
+
+        warm = keep.tile([P, 8], F32, name="warm")
+        nc.gpsimd.memset(warm[:], 0.0)
+        nc.scalar.activation(out=warm[:, 4:8], in_=warm[:, 0:4], func=ACT.Square)
+
+        windows = [keep.tile([P, T], F32, name=f"window{c}") for c in range(BLOCKS)]
+        for c in range(BLOCKS):
+            nc.gpsimd.memset(windows[c][:], 0.0)
+
+        picked = keep.tile([P, PACK, S], F32, name="picked")
+        x_bf = keep.tile([P, S, PACK], BF16, name="x_bf", align_bytes=64)
+        x_codes = keep.tile([P, S], U32, name="x_codes", align_bytes=64)
+        x_scales = keep.tile([P, S], U8, name="x_scales", align_bytes=64)
+        w_codes = [keep.tile([P, D * P], U32, name=f"w_codes{c}", align_bytes=64) for c in range(BLOCKS)]
+        w_scales = [keep.tile([P, D * P], U8, name=f"w_scales{c}", align_bytes=64) for c in range(BLOCKS)]
+        y = [keep.tile([P, V], F32, name=f"y{c}") for c in range(BLOCKS)]
+
+        def gather(j, a, z):
+            nc.vector.tensor_copy(out=picked[:, j, a:z], in_=planes[j][:].indirect(entries(a, z)))
+
+        def quantise_x(a, z):
+            nc.vector.quantize_mx(
+                out=x_codes[:, a:z].bitcast(FP8X4),
+                scales=x_scales[:, a:z],
+                in_=x_bf[:, a:z, :].rearrange("p s j -> p (s j)"),
+            )
+
+        def quantise_w(c, a, source):
+            z = a + source.shape[1]
+            nc.vector.quantize_mx(
+                out=w_codes[c][:, a:z].bitcast(FP8X4),
+                scales=w_scales[c][:, a:z],
+                in_=source.rearrange("p m j -> p (m j)"),
+            )
+
+        def w_tile(width, name, tag):
+            return work.tile([P, width, PACK], BF16, name=name, tag=tag, align_bytes=64)
+
+        def product(c, a, z, name):
+            acc = psum.tile([P, z - a], F32, name=name)
+            for d in range(D):
+                m = slice(d * P, (d + 1) * P)
+                s = slice(d * V + a, d * V + z)
+                nc.tensor.matmul_mx(
+                    out=acc[:],
+                    lhsT=w_codes[c][:, m].bitcast(FP8X4),
+                    lhsT_scale=w_scales[c][:, m],
+                    rhs=x_codes[:, s].bitcast(FP8X4),
+                    rhs_scale=x_scales[:, s],
+                    start=(d == 0),
+                    stop=(d == D - 1),
+                )
+            relu = work.tile([P, z - a], F32, name="relu_" + name, tag=name, align_bytes=64)
+            nc.scalar.activation(out=relu[:], in_=acc[:], func=ACT.Relu, bias=bias[:, c : c + 1])
+            nc.scalar.activation(out=y[c][:, a:z], in_=relu[:], func=ACT.Square)
+
+        def scatter(c, a, z, values):
+            nc.vector.tensor_tensor(
+                out=windows[c][:].indirect(entries(a, z)), in0=values, in1=gates[:, c, a:z], op=MULT
+            )
+
+        def piece(d, h):
+            return d * V + h * HALF, d * V + (h + 1) * HALF
+
+        def x_views(d, h):
+            a, z = piece(d, h)
+            return x_bf[:, a:z, :], picked[:, :, a:z]
+
+        w0 = w_tile(D * P, "w_bf0", "w_bf0")
+        last = PACK - 1
+        for j in range(last):
+            gather(j, 0, S)
+        gather(last, *piece(0, 0))
+        gather(last, *piece(1, 0))
+        gather(last, *piece(0, 1))
+        interleave_scalar(nc, *x_views(0, 0))
+        interleave_scalar(nc, w0[:, 0:P, :], w_source(0, 0))
+        interleave_vector(nc, *x_views(1, 0))
+        quantise_x(*piece(0, 0))
+        gather(last, *piece(1, 1))
+        interleave_scalar(nc, w0[:, P:, :], w_source(0, 1))
+        quantise_x(*piece(1, 0))
+        quantise_w(0, 0, w0[:, 0:P, :])
+        quantise_w(0, P, w0[:, P:, :])
+        interleave_scalar(nc, *x_views(0, 1))
+        interleave_vector(nc, *x_views(1, 1))
+        product(0, 0, HALF, "acc0a")
+        quantise_x(*piece(0, 1))
+        quantise_x(*piece(1, 1))
+        product(0, HALF, V, "acc0b")
+
+        def store(c):
+            nc.sync.dma_start(out=out[c * P : (c + 1) * P, :], in_=windows[c][:])
+
+        def cast_w(c, tag):
+            t = w_tile(D * P, f"w_bf{c}", tag)
+            for d in range(D):
+                interleave_scalar(nc, t[:, d * P : (d + 1) * P, :], w_source(c, d))
+            return t
+
+        w10 = w_tile(P, "w_bf10", "w_bf10")
+        interleave_scalar(nc, w10[:], w_source(1, 0))
+        w11 = w_tile(P, "w_bf11", "acc0a")
+        interleave_scalar(nc, w11[:], w_source(1, 1))
+        quantise_w(1, 0, w10[:])
+        scatter(0, 0, HALF, y[0][:, 0:HALF])
+        scatter(0, HALF, V, y[0][:, HALF:V])
+        quantise_w(1, P, w11[:])
+        product(1, 0, V, "acc1")
+        w2 = cast_w(2, "acc0b")
+        scatter(0, V, S, y[0][:])
+        store(0)
+        quantise_w(2, 0, w2[:])
+        product(2, 0, V, "acc2")
+        w3 = cast_w(3, "acc1")
+        scatter(1, 0, V, y[1][:])
+        quantise_w(3, 0, w3[:])
+        product(3, 0, V, "acc3")
+        scatter(1, V, S, y[1][:])
+        store(1)
+        scatter(2, 0, V, y[2][:])
+        scatter(3, 0, V, y[3][:])
+        scatter(2, V, S, y[2][:])
+        store(2)
+        scatter(3, V, S, y[3][:])
+        store(3)

@@ -13,6 +13,8 @@ U8 = mybir.dt.uint8
 FP8X4 = mybir.dt.float8_e4m3fn_x4
 ACT = mybir.ActivationFunctionType
 MULT = mybir.AluOpType.mult
+ADD = mybir.AluOpType.add
+MAX = mybir.AluOpType.max
 
 P = 128
 PACK = 4
@@ -48,36 +50,49 @@ def tile_picked_tome_lin_relu2_sub_e_kernel(tc, xT, w, b, gate, offs, out):
         offsets = keep.tile([P, S // PER_COL], U16, name="offsets")
         nc.sync.dma_start(offsets[:], offs)
 
+        bias = keep.tile([P, BLOCKS], F32, name="bias")
+        with nc.allow_non_contiguous_dma(reason="one bias value a partition"):
+            nc.scalar.dma_start(out=bias[:], in_=b.rearrange("(c p) o -> p (c o)", p=P))
+
         def entries(a, z):
             return offsets[:, a // PER_COL : z // PER_COL]
 
         x_rows = xT.rearrange("(p j) t -> p j t", j=PACK)
         planes = [keep.tile([P, T], F32, name=f"plane{j}") for j in range(PACK)]
+
+        w_rows = [w[d].rearrange("(p j) m -> p j m", j=PACK) for d in range(D)]
+        w_raw = [[keep.tile([P, PACK, P], F32, name=f"w_raw{c}_{d}") for d in range(D)] for c in range(BLOCKS)]
+        gates = keep.tile([P, BLOCKS, S], F32, name="gates")
+        gate_rows = gate.rearrange("(c p) s -> p c s", p=P)
+
         for j in range(PACK):
             nc.sync.dma_start(out=planes[j][:], in_=x_rows[:, j, :])
 
-        w_rows = [w[d].rearrange("(p j) m -> p j m", j=PACK) for d in range(D)]
-        w_raw = [[keep.tile([P, PACK, P], F32, name=f"w_raw{c}_{d}") for d in range(D)] for c in range(2)]
-        w_late = [keep.tile([P, PACK, 2 * P], F32, name=f"w_late{d}") for d in range(D)]
-        gates = keep.tile([P, BLOCKS, S], F32, name="gates")
-        gate_rows = gate.rearrange("(c p) s -> p c s", p=P)
-        bias = keep.tile([P, BLOCKS], F32, name="bias")
+        def load_w(c, d):
+            nc.sync.dma_start(out=w_raw[c][d][:], in_=w_rows[d][:, :, c * P : (c + 1) * P])
 
-        for d in range(D):
-            nc.sync.dma_start(out=w_raw[0][d][:], in_=w_rows[d][:, :, 0:P])
-        with nc.allow_non_contiguous_dma(reason="one bias value a partition"):
-            nc.sync.dma_start(out=bias[:], in_=b.rearrange("(c p) o -> p (c o)", p=P))
-        for d in range(D):
-            nc.sync.dma_start(out=w_raw[1][d][:], in_=w_rows[d][:, :, P : 2 * P])
-            nc.sync.dma_start(out=gates[:, 0, d * V : (d + 1) * V], in_=gate_rows[:, 0, d * V : (d + 1) * V])
-        for d in range(D):
-            nc.sync.dma_start(out=w_late[d][:], in_=w_rows[d][:, :, 2 * P : 4 * P])
-        nc.sync.dma_start(out=gates[:, 1:4, :], in_=gate_rows[:, 1:4, :])
+        def load_gate_half(h):
+            cols = slice(h * HALF, (h + 1) * HALF)
+            nc.sync.dma_start(
+                out=gates[:, 0, :].rearrange("p (d v) -> p d v", d=D)[:, :, cols],
+                in_=gate_rows[:, 0, :].rearrange("p (d v) -> p d v", d=D)[:, :, cols],
+            )
+
+        load_w(0, 0)
+        load_w(0, 1)
+        load_w(1, 0)
+        load_w(1, 1)
+        load_gate_half(0)
+        load_w(2, 0)
+        load_gate_half(1)
+        load_w(2, 1)
+        load_w(3, 0)
+        nc.sync.dma_start(out=gates[:, 1, :], in_=gate_rows[:, 1, :])
+        load_w(3, 1)
+        nc.sync.dma_start(out=gates[:, 2:4, :], in_=gate_rows[:, 2:4, :])
 
         def w_source(c, d):
-            if c < 2:
-                return w_raw[c][d][:]
-            return w_late[d][:, :, (c - 2) * P : (c - 1) * P]
+            return w_raw[c][d][:]
 
         warm = keep.tile([P, 8], F32, name="warm")
         nc.gpsimd.memset(warm[:], 0.0)
@@ -130,6 +145,17 @@ def tile_picked_tome_lin_relu2_sub_e_kernel(tc, xT, w, b, gate, offs, out):
                     start=(d == 0),
                     stop=(d == D - 1),
                 )
+            return acc
+
+        def square_relu_vector(c, a, z, acc):
+            relu = work.tile([P, z - a], F32, name="relu_first")
+            nc.vector.tensor_scalar(
+                out=relu[:], in0=acc[:], scalar1=bias[:, c : c + 1], scalar2=0.0, op0=ADD, op1=MAX
+            )
+            nc.vector.tensor_tensor(out=y[c][:, a:z], in0=relu[:], in1=relu[:], op=MULT)
+
+        def square_relu(c, a, z, name):
+            acc = product(c, a, z, name)
             relu = work.tile([P, z - a], F32, name="relu_" + name, tag=name, align_bytes=64)
             nc.scalar.activation(out=relu[:], in_=acc[:], func=ACT.Relu, bias=bias[:, c : c + 1])
             nc.scalar.activation(out=y[c][:, a:z], in_=relu[:], func=ACT.Square)
@@ -145,6 +171,15 @@ def tile_picked_tome_lin_relu2_sub_e_kernel(tc, xT, w, b, gate, offs, out):
         def x_views(d, h):
             a, z = piece(d, h)
             return x_bf[:, a:z, :], picked[:, :, a:z]
+
+        def store(c):
+            nc.sync.dma_start(out=out[c * P : (c + 1) * P, :], in_=windows[c][:])
+
+        def cast_w(c, tag):
+            t = w_tile(D * P, f"w_bf{c}", tag)
+            for d in range(D):
+                interleave_scalar(nc, t[:, d * P : (d + 1) * P, :], w_source(c, d))
+            return t
 
         w0 = w_tile(D * P, "w_bf0", "w_bf0")
         last = PACK - 1
@@ -163,39 +198,21 @@ def tile_picked_tome_lin_relu2_sub_e_kernel(tc, xT, w, b, gate, offs, out):
         quantise_w(0, 0, w0[:, 0:P, :])
         quantise_w(0, P, w0[:, P:, :])
         interleave_scalar(nc, *x_views(0, 1))
+        square_relu_vector(0, 0, HALF, product(0, 0, HALF, "acc0a"))
         interleave_vector(nc, *x_views(1, 1))
-        product(0, 0, HALF, "acc0a")
         quantise_x(*piece(0, 1))
         quantise_x(*piece(1, 1))
-        product(0, HALF, V, "acc0b")
+        square_relu(0, HALF, V, "acc0b")
+        for c in range(1, BLOCKS):
+            quantise_w(c, 0, cast_w(c, f"w_bf{c}")[:])
+            square_relu(c, 0, V, f"acc{c}")
 
-        def store(c):
-            nc.sync.dma_start(out=out[c * P : (c + 1) * P, :], in_=windows[c][:])
-
-        def cast_w(c, tag):
-            t = w_tile(D * P, f"w_bf{c}", tag)
-            for d in range(D):
-                interleave_scalar(nc, t[:, d * P : (d + 1) * P, :], w_source(c, d))
-            return t
-
-        w10 = w_tile(P, "w_bf10", "w_bf10")
-        interleave_scalar(nc, w10[:], w_source(1, 0))
-        w11 = w_tile(P, "w_bf11", "acc0a")
-        interleave_scalar(nc, w11[:], w_source(1, 1))
-        quantise_w(1, 0, w10[:])
         scatter(0, 0, HALF, y[0][:, 0:HALF])
+        scatter(0, V, V + HALF, y[0][:, 0:HALF])
         scatter(0, HALF, V, y[0][:, HALF:V])
-        quantise_w(1, P, w11[:])
-        product(1, 0, V, "acc1")
-        w2 = cast_w(2, "acc0b")
-        scatter(0, V, S, y[0][:])
+        scatter(0, V + HALF, S, y[0][:, HALF:V])
         store(0)
-        quantise_w(2, 0, w2[:])
-        product(2, 0, V, "acc2")
-        w3 = cast_w(3, "acc1")
         scatter(1, 0, V, y[1][:])
-        quantise_w(3, 0, w3[:])
-        product(3, 0, V, "acc3")
         scatter(1, V, S, y[1][:])
         store(1)
         scatter(2, 0, V, y[2][:])

@@ -1,6 +1,7 @@
 from contextlib import ExitStack
 
 import concourse.mybir as mybir
+from concourse.masks import make_identity
 
 K, T, D, S, V, N = 512, 1024, 2, 512, 256, 512
 FLOPS = 2 * D * K * N * V
@@ -12,9 +13,7 @@ U16 = mybir.dt.uint16
 U8 = mybir.dt.uint8
 FP8X4 = mybir.dt.float8_e4m3fn_x4
 ACT = mybir.ActivationFunctionType
-MULT = mybir.AluOpType.mult
-ADD = mybir.AluOpType.add
-MAX = mybir.AluOpType.max
+ALU = mybir.AluOpType
 
 P = 128
 PACK = 4
@@ -40,6 +39,12 @@ def interleave_vector(nc, dst, src):
     nc.vector.tensor_copy(out=o, in_=i)
 
 
+def quantise(nc, codes, scales, values):
+    nc.vector.quantize_mx(
+        out=codes.bitcast(FP8X4), scales=scales, in_=values.rearrange("p c j -> p (c j)")
+    )
+
+
 def tile_picked_tome_lin_relu2_sub_e_kernel(tc, xT, w, b, gate, offs, out):
     nc = tc.nc
     with ExitStack() as ctx:
@@ -48,94 +53,90 @@ def tile_picked_tome_lin_relu2_sub_e_kernel(tc, xT, w, b, gate, offs, out):
         psum = ctx.enter_context(tc.psum_pool(name="psum", bufs=1))
 
         offsets = keep.tile([P, S // PER_COL], U16, name="offsets")
-        nc.sync.dma_start(offsets[:], offs)
-
-        bias = keep.tile([P, BLOCKS], F32, name="bias")
-        with nc.allow_non_contiguous_dma(reason="one bias value a partition"):
-            nc.scalar.dma_start(out=bias[:], in_=b.rearrange("(c p) o -> p (c o)", p=P))
-
-        def entries(a, z):
-            return offsets[:, a // PER_COL : z // PER_COL]
-
-        x_rows = xT.rearrange("(p j) t -> p j t", j=PACK)
         planes = [keep.tile([P, T], F32, name=f"plane{j}") for j in range(PACK)]
-
-        w_rows = [w[d].rearrange("(p j) m -> p j m", j=PACK) for d in range(D)]
-        w_raw = [[keep.tile([P, PACK, P], F32, name=f"w_raw{c}_{d}") for d in range(D)] for c in range(BLOCKS)]
+        w_raw = [
+            [work.tile([P, PACK, P], F32, name=f"w_raw{c}_{d}", tag=f"w_raw{c}_{d}") for d in range(D)]
+            for c in range(BLOCKS)
+        ]
         gates = keep.tile([P, BLOCKS, S], F32, name="gates")
+        x_rows = xT.rearrange("(p j) t -> p j t", j=PACK)
+        w_rows = [w[d].rearrange("(p j) m -> p j m", j=PACK) for d in range(D)]
         gate_rows = gate.rearrange("(c p) s -> p c s", p=P)
-
-        for j in range(PACK):
-            nc.sync.dma_start(out=planes[j][:], in_=x_rows[:, j, :])
 
         def load_w(c, d):
             nc.sync.dma_start(out=w_raw[c][d][:], in_=w_rows[d][:, :, c * P : (c + 1) * P])
 
-        def load_gate_half(h):
+        def load_first_gate(h):
             cols = slice(h * HALF, (h + 1) * HALF)
             nc.sync.dma_start(
                 out=gates[:, 0, :].rearrange("p (d v) -> p d v", d=D)[:, :, cols],
                 in_=gate_rows[:, 0, :].rearrange("p (d v) -> p d v", d=D)[:, :, cols],
             )
 
-        load_w(0, 0)
-        load_w(0, 1)
-        load_w(1, 0)
-        load_w(1, 1)
-        load_gate_half(0)
+        nc.sync.dma_start(out=planes[0][:], in_=x_rows[:, 0, :])
+        nc.sync.dma_start(offsets[:], offs)
+        for j in range(1, PACK):
+            nc.sync.dma_start(out=planes[j][:], in_=x_rows[:, j, :])
+        for c in range(2):
+            for d in range(D):
+                load_w(c, d)
+        load_first_gate(0)
         load_w(2, 0)
-        load_gate_half(1)
+        load_first_gate(1)
         load_w(2, 1)
         load_w(3, 0)
-        nc.sync.dma_start(out=gates[:, 1, :], in_=gate_rows[:, 1, :])
         load_w(3, 1)
-        nc.sync.dma_start(out=gates[:, 2:4, :], in_=gate_rows[:, 2:4, :])
+        nc.sync.dma_start(out=gates[:, 1, :], in_=gate_rows[:, 1, :])
+        nc.sync.dma_start(out=gates[:, 2:, :], in_=gate_rows[:, 2:, :])
 
-        def w_source(c, d):
-            return w_raw[c][d][:]
-
+        bias_rows = keep.tile([P, P], F32, name="bias_rows")
+        identity = keep.tile([P, P], F32, name="identity")
+        bias = keep.tile([P, BLOCKS], F32, name="bias")
+        nc.gpsimd.memset(bias_rows[:], 0.0)
+        nc.scalar.dma_start(out=bias_rows[0:BLOCKS, :], in_=b.rearrange("(c p) o -> c (p o)", p=P))
+        make_identity(nc, identity[:])
         warm = keep.tile([P, 8], F32, name="warm")
-        nc.gpsimd.memset(warm[:], 0.0)
-        nc.scalar.activation(out=warm[:, 4:8], in_=warm[:, 0:4], func=ACT.Square)
+        nc.scalar.activation(out=warm[:], in_=identity[:, 0:8], func=ACT.Square)
+        bias_turned = psum.tile([P, P], F32, name="bias_turned")
+        nc.tensor.transpose(bias_turned[:], bias_rows[:], identity[:])
+        nc.scalar.activation(out=bias[:], in_=bias_turned[:, 0:BLOCKS], func=ACT.Copy)
 
         windows = [keep.tile([P, T], F32, name=f"window{c}") for c in range(BLOCKS)]
-        for c in range(BLOCKS):
-            nc.gpsimd.memset(windows[c][:], 0.0)
+        for c in range(BLOCKS - 1):
+            nc.vector.memset(windows[c][:], 0.0)
+        nc.gpsimd.memset(windows[BLOCKS - 1][:], 0.0)
 
         picked = keep.tile([P, PACK, S], F32, name="picked")
         x_bf = keep.tile([P, S, PACK], BF16, name="x_bf", align_bytes=64)
         x_codes = keep.tile([P, S], U32, name="x_codes", align_bytes=64)
         x_scales = keep.tile([P, S], U8, name="x_scales", align_bytes=64)
+        w_bf = [keep.tile([P, D * P, PACK], BF16, name=f"w_bf{c}", align_bytes=64) for c in range(BLOCKS)]
         w_codes = [keep.tile([P, D * P], U32, name=f"w_codes{c}", align_bytes=64) for c in range(BLOCKS)]
         w_scales = [keep.tile([P, D * P], U8, name=f"w_scales{c}", align_bytes=64) for c in range(BLOCKS)]
-        y = [keep.tile([P, V], F32, name=f"y{c}") for c in range(BLOCKS)]
 
-        def gather(j, a, z):
-            nc.vector.tensor_copy(out=picked[:, j, a:z], in_=planes[j][:].indirect(entries(a, z)))
+        def entries(d, h):
+            return slice(d * V + h * HALF, d * V + (h + 1) * HALF)
 
-        def quantise_x(a, z):
-            nc.vector.quantize_mx(
-                out=x_codes[:, a:z].bitcast(FP8X4),
-                scales=x_scales[:, a:z],
-                in_=x_bf[:, a:z, :].rearrange("p s j -> p (s j)"),
-            )
+        def listed(window, s):
+            return window[:].indirect(offsets[:, s.start // PER_COL : s.stop // PER_COL])
 
-        def quantise_w(c, a, source):
-            z = a + source.shape[1]
-            nc.vector.quantize_mx(
-                out=w_codes[c][:, a:z].bitcast(FP8X4),
-                scales=w_scales[c][:, a:z],
-                in_=source.rearrange("p m j -> p (m j)"),
-            )
+        def gather(j, s):
+            nc.vector.tensor_copy(out=picked[:, j, s], in_=listed(planes[j], s))
 
-        def w_tile(width, name, tag):
-            return work.tile([P, width, PACK], BF16, name=name, tag=tag, align_bytes=64)
+        def quantise_x(s):
+            quantise(nc, x_codes[:, s], x_scales[:, s], x_bf[:, s, :])
 
-        def product(c, a, z, name):
-            acc = psum.tile([P, z - a], F32, name=name)
+        def cast_w(c, d):
+            interleave_scalar(nc, w_bf[c][:, d * P : (d + 1) * P, :], w_raw[c][d][:])
+
+        def quantise_w(c, m):
+            quantise(nc, w_codes[c][:, m], w_scales[c][:, m], w_bf[c][:, m, :])
+
+        def product(c, groups, name):
+            acc = psum.tile([P, groups.stop - groups.start], F32, name=name)
             for d in range(D):
                 m = slice(d * P, (d + 1) * P)
-                s = slice(d * V + a, d * V + z)
+                s = slice(d * V + groups.start, d * V + groups.stop)
                 nc.tensor.matmul_mx(
                     out=acc[:],
                     lhsT=w_codes[c][:, m].bitcast(FP8X4),
@@ -147,77 +148,67 @@ def tile_picked_tome_lin_relu2_sub_e_kernel(tc, xT, w, b, gate, offs, out):
                 )
             return acc
 
-        def square_relu_vector(c, a, z, acc):
-            relu = work.tile([P, z - a], F32, name="relu_first")
-            nc.vector.tensor_scalar(
-                out=relu[:], in0=acc[:], scalar1=bias[:, c : c + 1], scalar2=0.0, op0=ADD, op1=MAX
-            )
-            nc.vector.tensor_tensor(out=y[c][:, a:z], in0=relu[:], in1=relu[:], op=MULT)
-
-        def square_relu(c, a, z, name):
-            acc = product(c, a, z, name)
-            relu = work.tile([P, z - a], F32, name="relu_" + name, tag=name, align_bytes=64)
+        def relu_scalar(c, acc, tag):
+            relu = work.tile([P, acc.shape[1]], F32, name=f"relu{c}", tag=tag)
             nc.scalar.activation(out=relu[:], in_=acc[:], func=ACT.Relu, bias=bias[:, c : c + 1])
-            nc.scalar.activation(out=y[c][:, a:z], in_=relu[:], func=ACT.Square)
+            return relu
 
-        def scatter(c, a, z, values):
-            nc.vector.tensor_tensor(
-                out=windows[c][:].indirect(entries(a, z)), in0=values, in1=gates[:, c, a:z], op=MULT
-            )
-
-        def piece(d, h):
-            return d * V + h * HALF, d * V + (h + 1) * HALF
-
-        def x_views(d, h):
-            a, z = piece(d, h)
-            return x_bf[:, a:z, :], picked[:, :, a:z]
+        def scatter(c, s, values):
+            nc.vector.tensor_tensor(out=listed(windows[c], s), in0=values, in1=gates[:, c, s], op=ALU.mult)
 
         def store(c):
             nc.sync.dma_start(out=out[c * P : (c + 1) * P, :], in_=windows[c][:])
 
-        def cast_w(c, tag):
-            t = w_tile(D * P, f"w_bf{c}", tag)
-            for d in range(D):
-                interleave_scalar(nc, t[:, d * P : (d + 1) * P, :], w_source(c, d))
-            return t
-
-        w0 = w_tile(D * P, "w_bf0", "w_bf0")
         last = PACK - 1
         for j in range(last):
-            gather(j, 0, S)
-        gather(last, *piece(0, 0))
-        gather(last, *piece(1, 0))
-        gather(last, *piece(0, 1))
-        interleave_scalar(nc, *x_views(0, 0))
-        interleave_scalar(nc, w0[:, 0:P, :], w_source(0, 0))
-        interleave_vector(nc, *x_views(1, 0))
-        quantise_x(*piece(0, 0))
-        gather(last, *piece(1, 1))
-        interleave_scalar(nc, w0[:, P:, :], w_source(0, 1))
-        quantise_x(*piece(1, 0))
-        quantise_w(0, 0, w0[:, 0:P, :])
-        quantise_w(0, P, w0[:, P:, :])
-        interleave_scalar(nc, *x_views(0, 1))
-        square_relu_vector(0, 0, HALF, product(0, 0, HALF, "acc0a"))
-        interleave_vector(nc, *x_views(1, 1))
-        quantise_x(*piece(0, 1))
-        quantise_x(*piece(1, 1))
-        square_relu(0, HALF, V, "acc0b")
-        for c in range(1, BLOCKS):
-            quantise_w(c, 0, cast_w(c, f"w_bf{c}")[:])
-            square_relu(c, 0, V, f"acc{c}")
+            gather(j, slice(0, S))
+        gather(last, entries(0, 0))
+        gather(last, entries(1, 0))
+        gather(last, entries(0, 1))
+        interleave_scalar(nc, x_bf[:, entries(0, 0), :], picked[:, :, entries(0, 0)])
+        cast_w(0, 0)
+        interleave_vector(nc, x_bf[:, entries(1, 0), :], picked[:, :, entries(1, 0)])
+        quantise_x(entries(0, 0))
+        gather(last, entries(1, 1))
+        cast_w(0, 1)
+        quantise_x(entries(1, 0))
+        quantise_w(0, slice(0, P))
+        quantise_w(0, slice(P, D * P))
+        interleave_scalar(nc, x_bf[:, entries(0, 1), :], picked[:, :, entries(0, 1)])
 
-        scatter(0, 0, HALF, y[0][:, 0:HALF])
-        scatter(0, V, V + HALF, y[0][:, 0:HALF])
-        scatter(0, HALF, V, y[0][:, HALF:V])
-        scatter(0, V + HALF, S, y[0][:, HALF:V])
+        y_first = keep.tile([P, D, HALF], F32, name="y_first")
+        acc = product(0, slice(0, HALF), "acc0a")
+        relu = keep.tile([P, HALF], F32, name="relu_first")
+        nc.vector.tensor_scalar(
+            out=relu[:], in0=acc[:], scalar1=bias[:, 0:1], scalar2=0.0, op0=ALU.add, op1=ALU.max
+        )
+        nc.vector.tensor_tensor(out=y_first[:, 0, :], in0=relu[:], in1=relu[:], op=ALU.mult)
+
+        interleave_vector(nc, x_bf[:, entries(1, 1), :], picked[:, :, entries(1, 1)])
+        quantise_x(entries(0, 1))
+        quantise_x(entries(1, 1))
+        acc = product(0, slice(HALF, V), "acc0b")
+        for d in range(D):
+            cast_w(1, d)
+        quantise_w(1, slice(0, D * P))
+        relu = relu_scalar(0, acc, "w_raw1_1")
+        nc.scalar.activation(out=y_first[:, 1, :], in_=relu[:], func=ACT.Square)
+
+        y = {}
+        for c in range(1, BLOCKS):
+            acc = product(c, slice(0, V), f"acc{c}")
+            if c + 1 < BLOCKS:
+                for d in range(D):
+                    cast_w(c + 1, d)
+                quantise_w(c + 1, slice(0, D * P))
+            relu = relu_scalar(c, acc, f"w_raw{c + 1}_1")
+            y[c] = keep.tile([P, D, V], F32, name=f"y{c}")
+            nc.scalar.activation(out=y[c][:], in_=relu[:].unsqueeze(1).to_broadcast([P, D, V]), func=ACT.Square)
+
+        for h in range(2):
+            for d in range(D):
+                scatter(0, entries(d, h), y_first[:, h, :])
         store(0)
-        scatter(1, 0, V, y[1][:])
-        scatter(1, V, S, y[1][:])
-        store(1)
-        scatter(2, 0, V, y[2][:])
-        scatter(3, 0, V, y[3][:])
-        scatter(2, V, S, y[2][:])
-        store(2)
-        scatter(3, V, S, y[3][:])
-        store(3)
+        for c in range(1, BLOCKS):
+            scatter(c, slice(0, S), y[c][:].rearrange("p d v -> p (d v)"))
+            store(c)

from contextlib import ExitStack

import concourse.mybir as mybir
from concourse.masks import make_identity

K, T, D, S, V, N = 512, 1024, 2, 512, 256, 512
FLOPS = 2 * D * K * N * V

F32 = mybir.dt.float32
BF16 = mybir.dt.bfloat16
U32 = mybir.dt.uint32
U16 = mybir.dt.uint16
U8 = mybir.dt.uint8
FP8X4 = mybir.dt.float8_e4m3fn_x4
ACT = mybir.ActivationFunctionType
ALU = mybir.AluOpType

P = 128
PACK = 4
BLOCKS = N // P
HALF = V // 2
PER_COL = 16


def interleave_views(dst, src):
    return (
        dst.rearrange("p (c i) t -> p c t i", i=4),
        src.rearrange("p t (c i) -> p c t i", i=4),
    )


def interleave_scalar(nc, dst, src):
    o, i = interleave_views(dst, src)
    nc.scalar.activation(out=o, in_=i, func=ACT.Copy)


def interleave_vector(nc, dst, src):
    o, i = interleave_views(dst, src)
    nc.vector.tensor_copy(out=o, in_=i)


def quantise(nc, codes, scales, values):
    nc.vector.quantize_mx(
        out=codes.bitcast(FP8X4), scales=scales, in_=values.rearrange("p c j -> p (c j)")
    )


def tile_picked_tome_lin_relu2_sub_e_kernel(tc, xT, w, b, gate, offs, out):
    nc = tc.nc
    with ExitStack() as ctx:
        keep = ctx.enter_context(tc.tile_pool(name="keep", bufs=1))
        work = ctx.enter_context(tc.tile_pool(name="work", bufs=1))
        psum = ctx.enter_context(tc.psum_pool(name="psum", bufs=1))

        offsets = keep.tile([P, S // PER_COL], U16, name="offsets")
        planes = [keep.tile([P, T], F32, name=f"plane{j}") for j in range(PACK)]
        w_raw = [
            [work.tile([P, PACK, P], F32, name=f"w_raw{c}_{d}", tag=f"w_raw{c}_{d}") for d in range(D)]
            for c in range(BLOCKS)
        ]
        gates = keep.tile([P, BLOCKS, S], F32, name="gates")
        x_rows = xT.rearrange("(p j) t -> p j t", j=PACK)
        w_rows = [w[d].rearrange("(p j) m -> p j m", j=PACK) for d in range(D)]
        gate_rows = gate.rearrange("(c p) s -> p c s", p=P)

        def load_w(c, d):
            nc.sync.dma_start(out=w_raw[c][d][:], in_=w_rows[d][:, :, c * P : (c + 1) * P])

        def load_first_gate(h):
            cols = slice(h * HALF, (h + 1) * HALF)
            nc.sync.dma_start(
                out=gates[:, 0, :].rearrange("p (d v) -> p d v", d=D)[:, :, cols],
                in_=gate_rows[:, 0, :].rearrange("p (d v) -> p d v", d=D)[:, :, cols],
            )

        nc.sync.dma_start(out=planes[0][:], in_=x_rows[:, 0, :])
        nc.sync.dma_start(offsets[:], offs)
        for j in range(1, PACK):
            nc.sync.dma_start(out=planes[j][:], in_=x_rows[:, j, :])
        for c in range(2):
            for d in range(D):
                load_w(c, d)
        load_first_gate(0)
        load_w(2, 0)
        load_first_gate(1)
        load_w(2, 1)
        load_w(3, 0)
        load_w(3, 1)
        nc.sync.dma_start(out=gates[:, 1, :], in_=gate_rows[:, 1, :])
        nc.sync.dma_start(out=gates[:, 2:, :], in_=gate_rows[:, 2:, :])

        bias_rows = keep.tile([P, P], F32, name="bias_rows")
        identity = keep.tile([P, P], F32, name="identity")
        bias = keep.tile([P, BLOCKS], F32, name="bias")
        nc.gpsimd.memset(bias_rows[:], 0.0)
        nc.scalar.dma_start(out=bias_rows[0:BLOCKS, :], in_=b.rearrange("(c p) o -> c (p o)", p=P))
        make_identity(nc, identity[:])
        warm = keep.tile([P, 8], F32, name="warm")
        nc.scalar.activation(out=warm[:], in_=identity[:, 0:8], func=ACT.Square)
        bias_turned = psum.tile([P, P], F32, name="bias_turned")
        nc.tensor.transpose(bias_turned[:], bias_rows[:], identity[:])
        nc.scalar.activation(out=bias[:], in_=bias_turned[:, 0:BLOCKS], func=ACT.Copy)

        windows = [keep.tile([P, T], F32, name=f"window{c}") for c in range(BLOCKS)]
        for c in range(BLOCKS - 1):
            nc.vector.memset(windows[c][:], 0.0)
        nc.gpsimd.memset(windows[BLOCKS - 1][:], 0.0)

        picked = keep.tile([P, PACK, S], F32, name="picked")
        x_bf = keep.tile([P, S, PACK], BF16, name="x_bf", align_bytes=64)
        x_codes = keep.tile([P, S], U32, name="x_codes", align_bytes=64)
        x_scales = keep.tile([P, S], U8, name="x_scales", align_bytes=64)
        w_bf = [keep.tile([P, D * P, PACK], BF16, name=f"w_bf{c}", align_bytes=64) for c in range(BLOCKS)]
        w_codes = [keep.tile([P, D * P], U32, name=f"w_codes{c}", align_bytes=64) for c in range(BLOCKS)]
        w_scales = [keep.tile([P, D * P], U8, name=f"w_scales{c}", align_bytes=64) for c in range(BLOCKS)]

        def entries(d, h):
            return slice(d * V + h * HALF, d * V + (h + 1) * HALF)

        def listed(window, s):
            return window[:].indirect(offsets[:, s.start // PER_COL : s.stop // PER_COL])

        def gather(j, s):
            nc.vector.tensor_copy(out=picked[:, j, s], in_=listed(planes[j], s))

        def quantise_x(s):
            quantise(nc, x_codes[:, s], x_scales[:, s], x_bf[:, s, :])

        def cast_w(c, d):
            interleave_scalar(nc, w_bf[c][:, d * P : (d + 1) * P, :], w_raw[c][d][:])

        def quantise_w(c, m):
            quantise(nc, w_codes[c][:, m], w_scales[c][:, m], w_bf[c][:, m, :])

        def product(c, groups, name):
            acc = psum.tile([P, groups.stop - groups.start], F32, name=name)
            for d in range(D):
                m = slice(d * P, (d + 1) * P)
                s = slice(d * V + groups.start, d * V + groups.stop)
                nc.tensor.matmul_mx(
                    out=acc[:],
                    lhsT=w_codes[c][:, m].bitcast(FP8X4),
                    lhsT_scale=w_scales[c][:, m],
                    rhs=x_codes[:, s].bitcast(FP8X4),
                    rhs_scale=x_scales[:, s],
                    start=(d == 0),
                    stop=(d == D - 1),
                )
            return acc

        def relu_scalar(c, acc, tag):
            relu = work.tile([P, acc.shape[1]], F32, name=f"relu{c}", tag=tag)
            nc.scalar.activation(out=relu[:], in_=acc[:], func=ACT.Relu, bias=bias[:, c : c + 1])
            return relu

        def scatter(c, s, values):
            nc.vector.tensor_tensor(out=listed(windows[c], s), in0=values, in1=gates[:, c, s], op=ALU.mult)

        def store(c):
            nc.sync.dma_start(out=out[c * P : (c + 1) * P, :], in_=windows[c][:])

        last = PACK - 1
        for j in range(last):
            gather(j, slice(0, S))
        gather(last, entries(0, 0))
        gather(last, entries(1, 0))
        gather(last, entries(0, 1))
        interleave_scalar(nc, x_bf[:, entries(0, 0), :], picked[:, :, entries(0, 0)])
        cast_w(0, 0)
        interleave_vector(nc, x_bf[:, entries(1, 0), :], picked[:, :, entries(1, 0)])
        quantise_x(entries(0, 0))
        gather(last, entries(1, 1))
        cast_w(0, 1)
        quantise_x(entries(1, 0))
        quantise_w(0, slice(0, P))
        quantise_w(0, slice(P, D * P))
        interleave_scalar(nc, x_bf[:, entries(0, 1), :], picked[:, :, entries(0, 1)])

        y_first = keep.tile([P, D, HALF], F32, name="y_first")
        acc = product(0, slice(0, HALF), "acc0a")
        relu = keep.tile([P, HALF], F32, name="relu_first")
        nc.vector.tensor_scalar(
            out=relu[:], in0=acc[:], scalar1=bias[:, 0:1], scalar2=0.0, op0=ALU.add, op1=ALU.max
        )
        nc.vector.tensor_tensor(out=y_first[:, 0, :], in0=relu[:], in1=relu[:], op=ALU.mult)

        interleave_vector(nc, x_bf[:, entries(1, 1), :], picked[:, :, entries(1, 1)])
        quantise_x(entries(0, 1))
        quantise_x(entries(1, 1))
        acc = product(0, slice(HALF, V), "acc0b")
        for d in range(D):
            cast_w(1, d)
        quantise_w(1, slice(0, D * P))
        relu = relu_scalar(0, acc, "w_raw1_1")
        nc.scalar.activation(out=y_first[:, 1, :], in_=relu[:], func=ACT.Square)

        y = {}
        for c in range(1, BLOCKS):
            acc = product(c, slice(0, V), f"acc{c}")
            if c + 1 < BLOCKS:
                for d in range(D):
                    cast_w(c + 1, d)
                quantise_w(c + 1, slice(0, D * P))
            relu = relu_scalar(c, acc, f"w_raw{c + 1}_1")
            y[c] = keep.tile([P, D, V], F32, name=f"y{c}")
            nc.scalar.activation(out=y[c][:], in_=relu[:].unsqueeze(1).to_broadcast([P, D, V]), func=ACT.Square)

        for h in range(2):
            for d in range(D):
                scatter(0, entries(d, h), y_first[:, h, :])
        store(0)
        for c in range(1, BLOCKS):
            scatter(c, slice(0, S), y[c][:].rearrange("p d v -> p (d v)"))
            store(c)
